import numpy as np
import ml_dtypes


def mxq(x, axis, fmt="e4m3"):
    dtype, down = {"e4m3": (ml_dtypes.float8_e4m3fn, 7), "e5m2": (ml_dtypes.float8_e5m2, 14)}[fmt]
    v = np.moveaxis(np.asarray(x, np.float32).astype(ml_dtypes.bfloat16).astype(np.float64), axis, -1)
    blocks = v.reshape(v.shape[:-1] + (-1, 32))
    amax = np.abs(blocks).max(-1, keepdims=True)
    byte = np.maximum(np.where(amax > 0, np.frexp(amax)[1] - 1 + 127, 0) - down, 1)
    scale = np.exp2(byte - 127.0)
    codes = (blocks / scale).astype(np.float32).astype(dtype).astype(np.float64)
    return np.moveaxis((codes * scale).reshape(v.shape), -1, axis)


WIDE = False


def mx_kscale(k):
    if not WIDE:
        return np.ones(k)
    levels = np.array([30, -30])
    if k % 512:
        return np.exp2(np.random.permutation(np.resize(levels, k // 32))).repeat(32)
    a = np.empty((k // 512, 16))
    for p in range(k // 512):
        a[p, :8] = np.random.permutation(np.resize(levels, 8))
        for g in range(8):
            far = levels[np.abs(levels - a[p, g]) >= 10]
            a[p, g + 8] = far[np.random.randint(len(far))]
    return np.exp2(a.ravel()).repeat(32)


def f64(x):
    return np.asarray(x).astype(np.float64)


def striped(idx):
    return np.tile(np.asarray(idx).reshape(-1, 16).T, (8, 1)).astype(np.uint16)


def unstriped(offs):
    return offs[:16].T.reshape(-1).astype(np.int64)


E2M1 = np.array([0.0, 0.5, 1.0, 1.5, 2.0, 3.0, 4.0, 6.0, -0.0, -0.5, -1.0, -1.5, -2.0, -3.0, -4.0, -6.0])


def pack_weight(w, fmt):
    k, n = w.shape
    w = f64(np.asarray(w, np.float32).astype(ml_dtypes.bfloat16)).reshape(k // 32, 32, n)
    amax = np.abs(w).max(1)
    if fmt in ("e4m3", "e5m2"):
        byte = np.frexp(amax)[1] - 1 + 127 - (7 if fmt == "e4m3" else 14)
    else:
        mant, ex = np.frexp(amax / 6.0)
        byte = np.where(mant > 0.5, ex, ex - 1) + 127
    byte = np.clip(np.where(amax > 0, byte, 1), 1, 254)
    scaled = (w * np.exp2(127.0 - byte)[:, None, :]).reshape(k, n).astype(np.float32)
    by_word = np.ascontiguousarray(scaled.reshape(k // 512, 128, 4, n).transpose(0, 1, 3, 2))
    if fmt in ("e4m3", "e5m2"):
        words = by_word.astype(ml_dtypes.float8_e4m3fn if fmt == "e4m3" else ml_dtypes.float8_e5m2).view(np.uint8)
    else:
        c = by_word.astype(ml_dtypes.float4_e2m1fn).view(np.uint8) & 0xF
        words = (c[..., 0::2] | (c[..., 1::2] << 4)).reshape(k // 512, 128, 2 * n)
    return np.ascontiguousarray(words), np.ascontiguousarray(byte.astype(np.uint8).reshape(k // 512, 16, n))


def unpack_weight(words, scales, fmt):
    g, _, n = scales.shape
    words = np.ascontiguousarray(words).reshape(g, 128, n, -1)
    if fmt in ("e4m3", "e5m2"):
        vals = words.view(ml_dtypes.float8_e4m3fn if fmt == "e4m3" else ml_dtypes.float8_e5m2).astype(np.float64)
    else:
        nib = np.empty((g, 128, n, 4), np.uint8)
        nib[..., 0::2] = words & 0xF
        nib[..., 1::2] = words >> 4
        vals = E2M1[nib]
    vals = vals * np.repeat(np.exp2(scales.astype(np.float64) - 127.0), 8, axis=1)[..., None]
    return vals.transpose(0, 1, 3, 2).reshape(g * 512, n)


K, T, J, R, F, N, C = 512, 512, 256, 512, 512, 256, 512


def setup_inputs():
    n = np.random.standard_normal
    idx = np.random.permutation(T)[:J]
    idx2 = np.random.permutation(T)[:J]
    idx3 = np.random.permutation(C)[:J]
    fk = mx_kscale(K)
    fr = mx_kscale(R)
    ff = mx_kscale(F)
    wp = pack_weight(n((K, R)) * 1 / np.sqrt(K) * fk[:, None] * fr, "e2m1")
    sxp = pack_weight(n((F, J)) / ff[:, None], "e4m3")
    w2p = pack_weight(n((F, R)) * 1 / np.sqrt(F) * ff[:, None] * fr, "e5m2")
    wbp = pack_weight(n((R, N)) * 1 / np.sqrt(R) / fr[:, None], "e5m2")
    return {
        "xf": (n((K, T))).astype(np.float32),
        "fk": (np.random.uniform(0.5, 2.0, (K, 1)) / fk[:, None]).astype(np.float32),
        "w_words": wp[0],
        "w_scales": wp[1],
        "sx_words": sxp[0],
        "sx_scales": sxp[1],
        "w2_words": w2p[0],
        "w2_scales": w2p[1],
        "wb_words": wbp[0],
        "wb_scales": wbp[1],
        "tz": (n((N, C))).astype(np.float32),
        "offs": striped(idx),
        "offs2": striped(idx2),
        "offs3": striped(idx3),
    }


def reference(xf, fk, w_words, w_scales, sx_words, sx_scales, w2_words, w2_scales, wb_words, wb_scales, tz, offs, offs2, offs3):
    idx = unstriped(offs)
    idx2 = unstriped(offs2)
    idx3 = unstriped(offs3)
    wu = unpack_weight(w_words, w_scales, "e2m1")
    sxu = unpack_weight(sx_words, sx_scales, "e4m3")
    w2u = unpack_weight(w2_words, w2_scales, "e5m2")
    wbu = unpack_weight(wb_words, wb_scales, "e5m2")
    u = (f64(xf)[:, idx] - f64(xf)[:, idx2]) * f64(fk)
    uq = mxq(u, 0, "e4m3")
    a = wu.T @ uq + w2u.T @ sxu
    pk1 = np.max(a, axis=1, keepdims=True)
    hid = np.maximum(a - 0.4 * pk1, 0.0)
    hidq = mxq(hid, 0, "e5m2")
    p = wbu.T @ hidq
    y = p * f64(tz)[:, idx3]
    return y

@@ -1,0 +1,164 @@
+from contextlib import ExitStack
+
+import concourse.mybir as mybir
+
+K, T, J, R, F, N, C = 512, 512, 256, 512, 512, 256, 512
+FLOPS = 2 * K * R * J + 2 * F * R * J + 2 * R * N * J
+
+F32 = mybir.dt.float32
+BF16 = mybir.dt.bfloat16
+I32 = mybir.dt.int32
+U32 = mybir.dt.uint32
+U16 = mybir.dt.uint16
+U8 = mybir.dt.uint8
+E4M3 = mybir.dt.float8_e4m3fn_x4
+E5M2 = mybir.dt.float8_e5m2_x4
+E2M1 = mybir.dt.float4_e2m1fn_x4
+ALU = mybir.AluOpType
+ACT = mybir.ActivationFunctionType
+
+P = 128
+PACK = 4
+HALF = J // 2
+
+
+def load_scale_rows(queue, plane, scales):
+    for q in range(4):
+        queue.dma_start(out=plane[32 * q : 32 * q + 4, :].bitcast(I32), in_=scales[0, 4 * q : 4 * q + 4, :].bitcast(I32))
+
+
+def interleave(nc, grouped, planes, cols):
+    nc.vector.tensor_copy(
+        out=grouped[:, cols, :].rearrange("p (c i) t -> p c t i", i=4),
+        in_=planes[:, :, cols].rearrange("p t (c i) -> p c t i", i=4),
+    )
+
+
+def quantize(nc, codes, scales, grouped, cols, fmt):
+    nc.vector.quantize_mx(
+        out=codes[:, cols].bitcast(fmt),
+        scales=scales[:, cols],
+        in_=grouped[:, cols, :].rearrange("p j t -> p (j t)"),
+    )
+
+
+def tile_list_sum_pickgaps_own_peakgated_timeslook_kernel(
+    tc, xf, fk, w_words, w_scales, sx_words, sx_scales, w2_words, w2_scales, wb_words, wb_scales, tz, offs, offs2, offs3, out
+):
+    nc = tc.nc
+    halves = [slice(0, HALF), slice(HALF, J)]
+    with ExitStack() as ctx:
+        sb = ctx.enter_context(tc.tile_pool(name="sb", bufs=1))
+        ps = ctx.enter_context(tc.psum_pool(name="ps", bufs=1))
+
+        list1 = sb.tile([P, J // 16], U16, name="list1")
+        list2 = sb.tile([P, J // 16], U16, name="list2")
+        list3 = sb.tile([P, J // 16], U16, name="list3")
+        x_plane = [sb.tile([P, T], F32, name=f"x{t}") for t in range(PACK)]
+        fk_sb = sb.tile([P, PACK], F32, name="fk_sb")
+        w_raw = sb.tile([P, 2 * R], U8, name="w_raw", align_bytes=64)
+        w2_raw = sb.tile([P, R], U32, name="w2_raw", align_bytes=64)
+        ws_raw = sb.tile([P, 2 * R], U8, name="ws_raw", align_bytes=64)
+        sx_sb = sb.tile([P, J], U32, name="sx_sb", align_bytes=64)
+        wb_sb = sb.tile([P, N], U32, name="wb_sb", align_bytes=64)
+        sx_sc = sb.tile([P, J], U8, name="sx_sc", align_bytes=64)
+        wb_sc = sb.tile([P, N], U8, name="wb_sc", align_bytes=64)
+        tz_sb = sb.tile([P, 2, C], F32, name="tz_sb")
+
+        nc.vector.memset(ws_raw[:].bitcast(U32), 0)
+        nc.vector.memset(wb_sc[:].bitcast(U32), 0)
+        nc.vector.memset(sx_sc[:].bitcast(U32), 0)
+
+        x_rows = xf.rearrange("(p t) c -> p t c", t=PACK)
+        nc.sync.dma_start(list2[:], offs2)
+        nc.sync.dma_start(out=x_plane[0][:], in_=x_rows[:, 0, :])
+        nc.sync.dma_start(list1[:], offs)
+        for t in range(1, PACK):
+            nc.sync.dma_start(out=x_plane[t][:], in_=x_rows[:, t, :])
+        nc.gpsimd.dma_start(out=fk_sb[:], in_=fk.rearrange("(p t) o -> p (t o)", t=PACK))
+        load_scale_rows(nc.gpsimd, wb_sc, wb_scales)
+        nc.sync.dma_start(out=w2_raw[:].bitcast(I32), in_=w2_words[0].rearrange("p n t -> p (n t)").bitcast(I32))
+        nc.sync.dma_start(out=w_raw[:].bitcast(I32), in_=w_words[0].bitcast(I32))
+        load_scale_rows(nc.sync, ws_raw[:, 0:R], w_scales)
+        load_scale_rows(nc.sync, ws_raw[:, R : 2 * R], w2_scales)
+        nc.sync.dma_start(out=sx_sb[:].bitcast(I32), in_=sx_words[0].rearrange("p n t -> p (n t)").bitcast(I32))
+        load_scale_rows(nc.sync, sx_sc, sx_scales)
+        nc.sync.dma_start(out=tz_sb[:], in_=tz.rearrange("(h p) c -> p h c", p=P))
+        nc.sync.dma_start(list3[:], offs3)
+        nc.sync.dma_start(out=wb_sb[:].bitcast(I32), in_=wb_words[0].rearrange("p n t -> p (n t)").bitcast(I32))
+
+        second = [sb.tile([P, J], F32, name=f"second{t}") for t in range(PACK)]
+        gap = [sb.tile([P, J], F32, name=f"gap{t}") for t in range(PACK)]
+        u_planes = sb.tile([P, PACK, J], BF16, name="u_planes")
+        for t in range(PACK):
+            nc.scalar.activation(second[t][:], x_plane[t][:].indirect(list2[:]), ACT.Copy)
+        for t in range(PACK):
+            nc.vector.tensor_tensor(gap[t][:], x_plane[t][:].indirect(list1[:]), second[t][:], ALU.subtract)
+            nc.scalar.activation(u_planes[:, t, :], gap[t][:], ACT.Copy, scale=fk_sb[:, t : t + 1])
+
+        w_sc = sb.tile([P, PACK, 2 * P], U8, name="w_sc", align_bytes=64)
+        nc.vector.tensor_copy(
+            out=w_sc[:].rearrange("p t (c i) -> p c t i", i=16),
+            in_=ws_raw[:].rearrange("p (c i t) -> p c t i", i=16, t=PACK),
+        )
+        w2_sb = sb.tile([P, PACK, P], U32, name="w2_sb", align_bytes=64)
+        nc.scalar.copy(
+            out=w2_sb[:].rearrange("p t (c i) -> p c t i", i=4),
+            in_=w2_raw[:].rearrange("p (c i t) -> p c t i", i=4, t=PACK),
+        )
+        w_sb = sb.tile([P, PACK, 2 * P], U8, name="w_sb", align_bytes=64)
+        nc.scalar.copy(
+            out=w_sb[:].bitcast(U16).rearrange("p t (c i) -> p c t i", i=8),
+            in_=w_raw[:].bitcast(U16).rearrange("p (c i t) -> p c t i", i=8, t=PACK),
+        )
+
+        u_grouped = sb.tile([P, J, PACK], BF16, name="u_grouped", align_bytes=64)
+        u_codes = sb.tile([P, J], U32, name="u_codes", align_bytes=64)
+        u_sc = sb.tile([P, J], U8, name="u_sc", align_bytes=64)
+        for cols in halves:
+            interleave(nc, u_grouped, u_planes, cols)
+        for cols in halves:
+            quantize(nc, u_codes, u_sc, u_grouped, cols, E4M3)
+
+        a_bank = [ps.tile([P, J], F32, name=f"a{t}") for t in range(PACK)]
+        for t in range(PACK):
+            nc.tensor.matmul_mx(
+                out=a_bank[t][:], lhsT=w2_sb[:, t, :].bitcast(E5M2), lhsT_scale=w_sc[:, t, P : 2 * P],
+                rhs=sx_sb[:].bitcast(E4M3), rhs_scale=sx_sc[:], start=True, stop=False,
+            )
+        for t in range(PACK):
+            nc.tensor.matmul_mx(
+                out=a_bank[t][:], lhsT=w_sb[:, t, :].bitcast(E2M1), lhsT_scale=w_sc[:, t, 0:P],
+                rhs=u_codes[:].bitcast(E4M3), rhs_scale=u_sc[:], start=False, stop=True,
+            )
+
+        scaled = sb.tile([P, PACK, J], F32, name="scaled")
+        cut = [sb.tile([P, 1], F32, name=f"cut{t}") for t in range(PACK)]
+        h_planes = sb.tile([P, PACK, J], BF16, name="h_planes")
+        for t in range(PACK):
+            nc.vector.tensor_scalar(scaled[:, t, :], a_bank[t][:], -0.4, None, ALU.mult, ALU.min, accum_out=cut[t][:])
+            nc.scalar.activation(h_planes[:, t, :], a_bank[t][:], ACT.Relu, bias=cut[t][:])
+
+        picked = sb.tile([P, 2, J], F32, name="picked")
+        for h in range(2):
+            nc.scalar.activation(picked[:, h, :], tz_sb[:, h, :].indirect(list3[:]), ACT.Copy)
+
+        h_grouped = sb.tile([P, J, PACK], BF16, name="h_grouped", align_bytes=64)
+        h_codes = sb.tile([P, J], U32, name="h_codes", align_bytes=64)
+        h_sc = sb.tile([P, J], U8, name="h_sc", align_bytes=64)
+        for cols in halves:
+            interleave(nc, h_grouped, h_planes, cols)
+        for cols in halves:
+            quantize(nc, h_codes, h_sc, h_grouped, cols, E5M2)
+
+        out_rows = out.rearrange("(h p) j -> p h j", p=P)
+        for g, cols in enumerate(halves):
+            p_bank = ps.tile([P, 2, HALF], F32, name=f"p{g}")
+            for h in range(2):
+                nc.tensor.matmul_mx(
+                    out=p_bank[:, h, :], lhsT=wb_sb[:, h * P : (h + 1) * P].bitcast(E5M2), lhsT_scale=wb_sc[:, h * P : (h + 1) * P],
+                    rhs=h_codes[:, cols].bitcast(E5M2), rhs_scale=h_sc[:, cols], start=True, stop=True,
+                )
+            y = sb.tile([P, 2, HALF], F32, name=f"y{g}")
+            nc.vector.tensor_tensor(y[:], p_bank[:], picked[:, :, cols], ALU.mult)
+            nc.sync.dma_start(out=out_rows[:, :, cols], in_=y[:])

@@ -22,9 +22,15 @@ PACK = 4
 HALF = J // 2
 
 
-def load_scale_rows(queue, plane, scales):
-    for q in range(4):
-        queue.dma_start(out=plane[32 * q : 32 * q + 4, :].bitcast(I32), in_=scales[0, 4 * q : 4 * q + 4, :].bitcast(I32))
+def load_scale_rows(queue, plane, scales, q):
+    queue.dma_start(out=plane[32 * q : 32 * q + 4, :].bitcast(I32), in_=scales[0, 4 * q : 4 * q + 4, :].bitcast(I32))
+
+
+def deal(copy, dealt, raw, run):
+    copy(
+        out=dealt.rearrange("p t (c i) -> p c t i", i=run),
+        in_=raw.rearrange("p (c i t) -> p c t i", i=run, t=PACK),
+    )
 
 
 def interleave(nc, grouped, planes, cols):
@@ -58,61 +64,73 @@ def tile_list_sum_pickgaps_own_peakgated_timeslook_kernel(
         fk_sb = sb.tile([P, PACK], F32, name="fk_sb")
         w_raw = sb.tile([P, 2 * R], U8, name="w_raw", align_bytes=64)
         w2_raw = sb.tile([P, R], U32, name="w2_raw", align_bytes=64)
-        ws_raw = sb.tile([P, 2 * R], U8, name="ws_raw", align_bytes=64)
+        ws_raw = sb.tile([P, R], U8, name="ws_raw", tag="ws_raw", align_bytes=64)
+        w2s_raw = sb.tile([P, R], U8, name="w2s_raw", tag="w2s_raw", align_bytes=64)
         sx_sb = sb.tile([P, J], U32, name="sx_sb", align_bytes=64)
         wb_sb = sb.tile([P, N], U32, name="wb_sb", align_bytes=64)
         sx_sc = sb.tile([P, J], U8, name="sx_sc", align_bytes=64)
         wb_sc = sb.tile([P, N], U8, name="wb_sc", align_bytes=64)
         tz_sb = sb.tile([P, 2, C], F32, name="tz_sb")
 
-        nc.vector.memset(ws_raw[:].bitcast(U32), 0)
-        nc.vector.memset(wb_sc[:].bitcast(U32), 0)
-        nc.vector.memset(sx_sc[:].bitcast(U32), 0)
+        warm_in = sb.tile([P, 1], F32, name="warm_in")
+        warm_out = sb.tile([P, 1], F32, name="warm_out")
+        nc.vector.memset(warm_in[:], 0.0)
+        nc.scalar.activation(warm_out[:], warm_in[:], ACT.Copy)
+        for plane in (w2s_raw, ws_raw, sx_sc, wb_sc):
+            nc.vector.memset(plane[:].bitcast(U32), 0)
 
         x_rows = xf.rearrange("(p t) c -> p t c", t=PACK)
-        nc.sync.dma_start(list2[:], offs2)
-        nc.sync.dma_start(out=x_plane[0][:], in_=x_rows[:, 0, :])
         nc.sync.dma_start(list1[:], offs)
-        for t in range(1, PACK):
+        nc.sync.dma_start(list2[:], offs2)
+        for t in range(PACK - 1):
             nc.sync.dma_start(out=x_plane[t][:], in_=x_rows[:, t, :])
-        nc.gpsimd.dma_start(out=fk_sb[:], in_=fk.rearrange("(p t) o -> p (t o)", t=PACK))
-        load_scale_rows(nc.gpsimd, wb_sc, wb_scales)
+            load_scale_rows(nc.sync, w2s_raw, w2_scales, t)
+        load_scale_rows(nc.sync, w2s_raw, w2_scales, 3)
+        nc.sync.dma_start(out=x_plane[3][:], in_=x_rows[:, 3, :])
         nc.sync.dma_start(out=w2_raw[:].bitcast(I32), in_=w2_words[0].rearrange("p n t -> p (n t)").bitcast(I32))
         nc.sync.dma_start(out=w_raw[:].bitcast(I32), in_=w_words[0].bitcast(I32))
-        load_scale_rows(nc.sync, ws_raw[:, 0:R], w_scales)
-        load_scale_rows(nc.sync, ws_raw[:, R : 2 * R], w2_scales)
+        for q in range(4):
+            load_scale_rows(nc.sync, ws_raw, w_scales, q)
         nc.sync.dma_start(out=sx_sb[:].bitcast(I32), in_=sx_words[0].rearrange("p n t -> p (n t)").bitcast(I32))
-        load_scale_rows(nc.sync, sx_sc, sx_scales)
+        load_scale_rows(nc.sync, sx_sc, sx_scales, 2)
+        load_scale_rows(nc.sync, sx_sc, sx_scales, 3)
         nc.sync.dma_start(out=tz_sb[:], in_=tz.rearrange("(h p) c -> p h c", p=P))
         nc.sync.dma_start(list3[:], offs3)
         nc.sync.dma_start(out=wb_sb[:].bitcast(I32), in_=wb_words[0].rearrange("p n t -> p (n t)").bitcast(I32))
+        nc.gpsimd.dma_start(out=fk_sb[:], in_=fk.rearrange("(p t) o -> p (t o)", t=PACK))
+        for q in range(2):
+            load_scale_rows(nc.gpsimd, sx_sc, sx_scales, q)
+        for q in range(4):
+            load_scale_rows(nc.gpsimd, wb_sc, wb_scales, q)
 
+        last = PACK - 1
+        first = [sb.tile([P, J], F32, name=f"first{t}", tag=f"first{t}", align_bytes=64) for t in range(PACK)]
         second = [sb.tile([P, J], F32, name=f"second{t}") for t in range(PACK)]
-        gap = [sb.tile([P, J], F32, name=f"gap{t}") for t in range(PACK)]
         u_planes = sb.tile([P, PACK, J], BF16, name="u_planes")
         for t in range(PACK):
             nc.scalar.activation(second[t][:], x_plane[t][:].indirect(list2[:]), ACT.Copy)
-        for t in range(PACK):
-            nc.vector.tensor_tensor(gap[t][:], x_plane[t][:].indirect(list1[:]), second[t][:], ALU.subtract)
-            nc.scalar.activation(u_planes[:, t, :], gap[t][:], ACT.Copy, scale=fk_sb[:, t : t + 1])
-
-        w_sc = sb.tile([P, PACK, 2 * P], U8, name="w_sc", align_bytes=64)
-        nc.vector.tensor_copy(
-            out=w_sc[:].rearrange("p t (c i) -> p c t i", i=16),
-            in_=ws_raw[:].rearrange("p (c i t) -> p c t i", i=16, t=PACK),
-        )
+            if t < last:
+                nc.vector.tensor_copy(first[t][:], x_plane[t][:].indirect(list1[:]))
+            else:
+                nc.scalar.activation(first[t][:], x_plane[t][:].indirect(list1[:]), ACT.Copy)
+        w2_sc = sb.tile([P, PACK, P], U8, name="w2_sc", align_bytes=64)
+        deal(nc.vector.tensor_copy, w2_sc[:], w2s_raw[:], 16)
+        gap = sb.tile([P, PACK, J], F32, name="gap", tag="w2s_raw", align_bytes=64)
+        for t in range(last):
+            nc.vector.tensor_tensor(gap[:, t, :], first[t][:], second[t][:], ALU.subtract)
+        for t in range(last):
+            nc.vector.tensor_scalar(u_planes[:, t, :], gap[:, t, :], fk_sb[:, t : t + 1], None, ALU.mult)
+        nc.vector.tensor_tensor(gap[:, last, :], first[last][:], second[last][:], ALU.subtract)
+        w_sc = sb.tile([P, PACK, P], U8, name="w_sc", tag=f"first{last}", align_bytes=64)
+        deal(nc.vector.tensor_copy, w_sc[:], ws_raw[:], 16)
+        for cols in halves:
+            nc.vector.tensor_scalar(u_planes[:, last, cols], gap[:, last, cols], fk_sb[:, last:PACK], None, ALU.mult)
         w2_sb = sb.tile([P, PACK, P], U32, name="w2_sb", align_bytes=64)
-        nc.scalar.copy(
-            out=w2_sb[:].rearrange("p t (c i) -> p c t i", i=4),
-            in_=w2_raw[:].rearrange("p (c i t) -> p c t i", i=4, t=PACK),
-        )
         w_sb = sb.tile([P, PACK, 2 * P], U8, name="w_sb", align_bytes=64)
-        nc.scalar.copy(
-            out=w_sb[:].bitcast(U16).rearrange("p t (c i) -> p c t i", i=8),
-            in_=w_raw[:].bitcast(U16).rearrange("p (c i t) -> p c t i", i=8, t=PACK),
-        )
+        deal(nc.scalar.copy, w2_sb[:], w2_raw[:], 4)
+        deal(nc.scalar.copy, w_sb[:].bitcast(U16), w_raw[:].bitcast(U16), 8)
 
-        u_grouped = sb.tile([P, J, PACK], BF16, name="u_grouped", align_bytes=64)
+        u_grouped = sb.tile([P, J, PACK], BF16, name="u_grouped", tag="ws_raw", align_bytes=64)
         u_codes = sb.tile([P, J], U32, name="u_codes", align_bytes=64)
         u_sc = sb.tile([P, J], U8, name="u_sc", align_bytes=64)
         for cols in halves:
@@ -123,12 +141,12 @@ def tile_list_sum_pickgaps_own_peakgated_timeslook_kernel(
         a_bank = [ps.tile([P, J], F32, name=f"a{t}") for t in range(PACK)]
         for t in range(PACK):
             nc.tensor.matmul_mx(
-                out=a_bank[t][:], lhsT=w2_sb[:, t, :].bitcast(E5M2), lhsT_scale=w_sc[:, t, P : 2 * P],
+                out=a_bank[t][:], lhsT=w2_sb[:, t, :].bitcast(E5M2), lhsT_scale=w2_sc[:, t, :],
                 rhs=sx_sb[:].bitcast(E4M3), rhs_scale=sx_sc[:], start=True, stop=False,
             )
         for t in range(PACK):
             nc.tensor.matmul_mx(
-                out=a_bank[t][:], lhsT=w_sb[:, t, :].bitcast(E2M1), lhsT_scale=w_sc[:, t, 0:P],
+                out=a_bank[t][:], lhsT=w_sb[:, t, :].bitcast(E2M1), lhsT_scale=w_sc[:, t, :],
                 rhs=u_codes[:].bitcast(E4M3), rhs_scale=u_sc[:], start=False, stop=True,
             )
 
@@ -137,7 +155,11 @@ def tile_list_sum_pickgaps_own_peakgated_timeslook_kernel(
         h_planes = sb.tile([P, PACK, J], BF16, name="h_planes")
         for t in range(PACK):
             nc.vector.tensor_scalar(scaled[:, t, :], a_bank[t][:], -0.4, None, ALU.mult, ALU.min, accum_out=cut[t][:])
+        for t in range(2):
             nc.scalar.activation(h_planes[:, t, :], a_bank[t][:], ACT.Relu, bias=cut[t][:])
+        nc.vector.tensor_scalar(h_planes[:, 2, :], a_bank[2][:], cut[2][:], 0.0, ALU.add, ALU.max)
+        for cols in halves:
+            nc.vector.tensor_scalar(h_planes[:, last, cols], a_bank[last][:, cols], cut[last][:], 0.0, ALU.add, ALU.max)
 
         picked = sb.tile([P, 2, J], F32, name="picked")
         for h in range(2):

@@ -64,7 +64,7 @@ def tile_list_sum_pickgaps_own_peakgated_timeslook_kernel(
         fk_sb = sb.tile([P, PACK], F32, name="fk_sb")
         w_raw = sb.tile([P, 2 * R], U8, name="w_raw", align_bytes=64)
         w2_raw = sb.tile([P, R], U32, name="w2_raw", align_bytes=64)
-        ws_raw = sb.tile([P, R], U8, name="ws_raw", tag="ws_raw", align_bytes=64)
+        ws_raw = sb.tile([P, R], U8, name="ws_raw", align_bytes=64)
         w2s_raw = sb.tile([P, R], U8, name="w2s_raw", tag="w2s_raw", align_bytes=64)
         sx_sb = sb.tile([P, J], U32, name="sx_sb", align_bytes=64)
         wb_sb = sb.tile([P, N], U32, name="wb_sb", align_bytes=64)
@@ -80,31 +80,31 @@ def tile_list_sum_pickgaps_own_peakgated_timeslook_kernel(
             nc.vector.memset(plane[:].bitcast(U32), 0)
 
         x_rows = xf.rearrange("(p t) c -> p t c", t=PACK)
+        nc.sync.dma_start(out=x_plane[0][:], in_=x_rows[:, 0, :])
         nc.sync.dma_start(list1[:], offs)
         nc.sync.dma_start(list2[:], offs2)
-        for t in range(PACK - 1):
+        for t in range(1, PACK):
             nc.sync.dma_start(out=x_plane[t][:], in_=x_rows[:, t, :])
-            load_scale_rows(nc.sync, w2s_raw, w2_scales, t)
-        load_scale_rows(nc.sync, w2s_raw, w2_scales, 3)
-        nc.sync.dma_start(out=x_plane[3][:], in_=x_rows[:, 3, :])
+        for q in range(4):
+            load_scale_rows(nc.sync, w2s_raw, w2_scales, q)
         nc.sync.dma_start(out=w2_raw[:].bitcast(I32), in_=w2_words[0].rearrange("p n t -> p (n t)").bitcast(I32))
+        nc.sync.dma_start(out=sx_sb[:].bitcast(I32), in_=sx_words[0].rearrange("p n t -> p (n t)").bitcast(I32))
+        for q in range(2, 4):
+            load_scale_rows(nc.sync, sx_sc, sx_scales, q)
         nc.sync.dma_start(out=w_raw[:].bitcast(I32), in_=w_words[0].bitcast(I32))
         for q in range(4):
             load_scale_rows(nc.sync, ws_raw, w_scales, q)
-        nc.sync.dma_start(out=sx_sb[:].bitcast(I32), in_=sx_words[0].rearrange("p n t -> p (n t)").bitcast(I32))
-        load_scale_rows(nc.sync, sx_sc, sx_scales, 2)
-        load_scale_rows(nc.sync, sx_sc, sx_scales, 3)
         nc.sync.dma_start(out=tz_sb[:], in_=tz.rearrange("(h p) c -> p h c", p=P))
         nc.sync.dma_start(list3[:], offs3)
         nc.sync.dma_start(out=wb_sb[:].bitcast(I32), in_=wb_words[0].rearrange("p n t -> p (n t)").bitcast(I32))
+        for q in range(4):
+            load_scale_rows(nc.sync, wb_sc, wb_scales, q)
         nc.gpsimd.dma_start(out=fk_sb[:], in_=fk.rearrange("(p t) o -> p (t o)", t=PACK))
         for q in range(2):
             load_scale_rows(nc.gpsimd, sx_sc, sx_scales, q)
-        for q in range(4):
-            load_scale_rows(nc.gpsimd, wb_sc, wb_scales, q)
 
         last = PACK - 1
-        first = [sb.tile([P, J], F32, name=f"first{t}", tag=f"first{t}", align_bytes=64) for t in range(PACK)]
+        first = [sb.tile([P, J], F32, name=f"first{t}") for t in range(PACK)]
         second = [sb.tile([P, J], F32, name=f"second{t}") for t in range(PACK)]
         u_planes = sb.tile([P, PACK, J], BF16, name="u_planes")
         for t in range(PACK):
@@ -116,13 +116,10 @@ def tile_list_sum_pickgaps_own_peakgated_timeslook_kernel(
         w2_sc = sb.tile([P, PACK, P], U8, name="w2_sc", align_bytes=64)
         deal(nc.vector.tensor_copy, w2_sc[:], w2s_raw[:], 16)
         gap = sb.tile([P, PACK, J], F32, name="gap", tag="w2s_raw", align_bytes=64)
-        for t in range(last):
+        for t in range(PACK):
             nc.vector.tensor_tensor(gap[:, t, :], first[t][:], second[t][:], ALU.subtract)
         for t in range(last):
             nc.vector.tensor_scalar(u_planes[:, t, :], gap[:, t, :], fk_sb[:, t : t + 1], None, ALU.mult)
-        nc.vector.tensor_tensor(gap[:, last, :], first[last][:], second[last][:], ALU.subtract)
-        w_sc = sb.tile([P, PACK, P], U8, name="w_sc", tag=f"first{last}", align_bytes=64)
-        deal(nc.vector.tensor_copy, w_sc[:], ws_raw[:], 16)
         for cols in halves:
             nc.vector.tensor_scalar(u_planes[:, last, cols], gap[:, last, cols], fk_sb[:, last:PACK], None, ALU.mult)
         w2_sb = sb.tile([P, PACK, P], U32, name="w2_sb", align_bytes=64)
@@ -130,13 +127,15 @@ def tile_list_sum_pickgaps_own_peakgated_timeslook_kernel(
         deal(nc.scalar.copy, w2_sb[:], w2_raw[:], 4)
         deal(nc.scalar.copy, w_sb[:].bitcast(U16), w_raw[:].bitcast(U16), 8)
 
-        u_grouped = sb.tile([P, J, PACK], BF16, name="u_grouped", tag="ws_raw", align_bytes=64)
+        u_grouped = sb.tile([P, J, PACK], BF16, name="u_grouped", align_bytes=64)
         u_codes = sb.tile([P, J], U32, name="u_codes", align_bytes=64)
         u_sc = sb.tile([P, J], U8, name="u_sc", align_bytes=64)
         for cols in halves:
             interleave(nc, u_grouped, u_planes, cols)
         for cols in halves:
             quantize(nc, u_codes, u_sc, u_grouped, cols, E4M3)
+        w_sc = sb.tile([P, PACK, P], U8, name="w_sc", align_bytes=64)
+        deal(nc.vector.tensor_copy, w_sc[:], ws_raw[:], 16)
 
         a_bank = [ps.tile([P, J], F32, name=f"a{t}") for t in range(PACK)]
         for t in range(PACK):
@@ -145,10 +144,11 @@ def tile_list_sum_pickgaps_own_peakgated_timeslook_kernel(
                 rhs=sx_sb[:].bitcast(E4M3), rhs_scale=sx_sc[:], start=True, stop=False,
             )
         for t in range(PACK):
-            nc.tensor.matmul_mx(
-                out=a_bank[t][:], lhsT=w_sb[:, t, :].bitcast(E2M1), lhsT_scale=w_sc[:, t, :],
-                rhs=u_codes[:].bitcast(E4M3), rhs_scale=u_sc[:], start=False, stop=True,
-            )
+            for g, cols in enumerate(halves):
+                nc.tensor.matmul_mx(
+                    out=a_bank[t][:, cols], lhsT=w_sb[:, t, :].bitcast(E2M1), lhsT_scale=w_sc[:, t, :],
+                    rhs=u_codes[:, cols].bitcast(E4M3), rhs_scale=u_sc[:, cols], start=False, stop=(g == 1),
+                )
 
         scaled = sb.tile([P, PACK, J], F32, name="scaled")
         cut = [sb.tile([P, 1], F32, name=f"cut{t}") for t in range(PACK)]

@@ -106,7 +106,6 @@ def tile_list_sum_pickgaps_own_peakgated_timeslook_kernel(
         last = PACK - 1
         first = [sb.tile([P, J], F32, name=f"first{t}") for t in range(PACK)]
         second = [sb.tile([P, J], F32, name=f"second{t}") for t in range(PACK)]
-        u_planes = sb.tile([P, PACK, J], BF16, name="u_planes")
         for t in range(PACK):
             nc.scalar.activation(second[t][:], x_plane[t][:].indirect(list2[:]), ACT.Copy)
             if t < last:
@@ -116,12 +115,10 @@ def tile_list_sum_pickgaps_own_peakgated_timeslook_kernel(
         w2_sc = sb.tile([P, PACK, P], U8, name="w2_sc", align_bytes=64)
         deal(nc.vector.tensor_copy, w2_sc[:], w2s_raw[:], 16)
         gap = sb.tile([P, PACK, J], F32, name="gap", tag="w2s_raw", align_bytes=64)
-        for t in range(PACK):
-            nc.vector.tensor_tensor(gap[:, t, :], first[t][:], second[t][:], ALU.subtract)
         for t in range(last):
-            nc.vector.tensor_scalar(u_planes[:, t, :], gap[:, t, :], fk_sb[:, t : t + 1], None, ALU.mult)
+            nc.vector.tensor_tensor(gap[:, t, :], first[t][:], second[t][:], ALU.subtract)
         for cols in halves:
-            nc.vector.tensor_scalar(u_planes[:, last, cols], gap[:, last, cols], fk_sb[:, last:PACK], None, ALU.mult)
+            nc.vector.tensor_tensor(gap[:, last, cols], first[last][:, cols], second[last][:, cols], ALU.subtract)
         w2_sb = sb.tile([P, PACK, P], U32, name="w2_sb", align_bytes=64)
         w_sb = sb.tile([P, PACK, 2 * P], U8, name="w_sb", align_bytes=64)
         deal(nc.scalar.copy, w2_sb[:], w2_raw[:], 4)
@@ -131,7 +128,12 @@ def tile_list_sum_pickgaps_own_peakgated_timeslook_kernel(
         u_codes = sb.tile([P, J], U32, name="u_codes", align_bytes=64)
         u_sc = sb.tile([P, J], U8, name="u_sc", align_bytes=64)
         for cols in halves:
-            interleave(nc, u_grouped, u_planes, cols)
+            nc.vector.tensor_tensor(
+                u_grouped[:, cols, :].rearrange("p (c i) t -> p c t i", i=4),
+                gap[:, :, cols].rearrange("p t (c i) -> p c t i", i=4),
+                fk_sb[:].unsqueeze(1).unsqueeze(3).broadcast_to([P, HALF // 4, PACK, 4]),
+                ALU.mult,
+            )
         for cols in halves:
             quantize(nc, u_codes, u_sc, u_grouped, cols, E4M3)
         w_sc = sb.tile([P, PACK, P], U8, name="w_sc", align_bytes=64)

from contextlib import ExitStack

import concourse.mybir as mybir

K, T, J, R, F, N, C = 512, 512, 256, 512, 512, 256, 512
FLOPS = 2 * K * R * J + 2 * F * R * J + 2 * R * N * J

F32 = mybir.dt.float32
BF16 = mybir.dt.bfloat16
I32 = mybir.dt.int32
U32 = mybir.dt.uint32
U16 = mybir.dt.uint16
U8 = mybir.dt.uint8
E4M3 = mybir.dt.float8_e4m3fn_x4
E5M2 = mybir.dt.float8_e5m2_x4
E2M1 = mybir.dt.float4_e2m1fn_x4
ALU = mybir.AluOpType
ACT = mybir.ActivationFunctionType

P = 128
PACK = 4
HALF = J // 2


def load_scale_rows(queue, plane, scales, q):
    queue.dma_start(out=plane[32 * q : 32 * q + 4, :].bitcast(I32), in_=scales[0, 4 * q : 4 * q + 4, :].bitcast(I32))


def deal(copy, dealt, raw, run):
    copy(
        out=dealt.rearrange("p t (c i) -> p c t i", i=run),
        in_=raw.rearrange("p (c i t) -> p c t i", i=run, t=PACK),
    )


def interleave(nc, grouped, planes, cols):
    nc.vector.tensor_copy(
        out=grouped[:, cols, :].rearrange("p (c i) t -> p c t i", i=4),
        in_=planes[:, :, cols].rearrange("p t (c i) -> p c t i", i=4),
    )


def quantize(nc, codes, scales, grouped, cols, fmt):
    nc.vector.quantize_mx(
        out=codes[:, cols].bitcast(fmt),
        scales=scales[:, cols],
        in_=grouped[:, cols, :].rearrange("p j t -> p (j t)"),
    )


def tile_list_sum_pickgaps_own_peakgated_timeslook_kernel(
    tc, xf, fk, w_words, w_scales, sx_words, sx_scales, w2_words, w2_scales, wb_words, wb_scales, tz, offs, offs2, offs3, out
):
    nc = tc.nc
    halves = [slice(0, HALF), slice(HALF, J)]
    with ExitStack() as ctx:
        sb = ctx.enter_context(tc.tile_pool(name="sb", bufs=1))
        ps = ctx.enter_context(tc.psum_pool(name="ps", bufs=1))

        list1 = sb.tile([P, J // 16], U16, name="list1")
        list2 = sb.tile([P, J // 16], U16, name="list2")
        list3 = sb.tile([P, J // 16], U16, name="list3")
        x_plane = [sb.tile([P, T], F32, name=f"x{t}") for t in range(PACK)]
        fk_sb = sb.tile([P, PACK], F32, name="fk_sb")
        w_raw = sb.tile([P, 2 * R], U8, name="w_raw", align_bytes=64)
        w2_raw = sb.tile([P, R], U32, name="w2_raw", align_bytes=64)
        ws_raw = sb.tile([P, R], U8, name="ws_raw", align_bytes=64)
        w2s_raw = sb.tile([P, R], U8, name="w2s_raw", tag="w2s_raw", align_bytes=64)
        sx_sb = sb.tile([P, J], U32, name="sx_sb", align_bytes=64)
        wb_sb = sb.tile([P, N], U32, name="wb_sb", align_bytes=64)
        sx_sc = sb.tile([P, J], U8, name="sx_sc", align_bytes=64)
        wb_sc = sb.tile([P, N], U8, name="wb_sc", align_bytes=64)
        tz_sb = sb.tile([P, 2, C], F32, name="tz_sb")

        warm_in = sb.tile([P, 1], F32, name="warm_in")
        warm_out = sb.tile([P, 1], F32, name="warm_out")
        nc.vector.memset(warm_in[:], 0.0)
        nc.scalar.activation(warm_out[:], warm_in[:], ACT.Copy)
        for plane in (w2s_raw, ws_raw, sx_sc, wb_sc):
            nc.vector.memset(plane[:].bitcast(U32), 0)

        x_rows = xf.rearrange("(p t) c -> p t c", t=PACK)
        nc.sync.dma_start(out=x_plane[0][:], in_=x_rows[:, 0, :])
        nc.sync.dma_start(list1[:], offs)
        nc.sync.dma_start(list2[:], offs2)
        for t in range(1, PACK):
            nc.sync.dma_start(out=x_plane[t][:], in_=x_rows[:, t, :])
        for q in range(4):
            load_scale_rows(nc.sync, w2s_raw, w2_scales, q)
        nc.sync.dma_start(out=w2_raw[:].bitcast(I32), in_=w2_words[0].rearrange("p n t -> p (n t)").bitcast(I32))
        nc.sync.dma_start(out=sx_sb[:].bitcast(I32), in_=sx_words[0].rearrange("p n t -> p (n t)").bitcast(I32))
        for q in range(2, 4):
            load_scale_rows(nc.sync, sx_sc, sx_scales, q)
        nc.sync.dma_start(out=w_raw[:].bitcast(I32), in_=w_words[0].bitcast(I32))
        for q in range(4):
            load_scale_rows(nc.sync, ws_raw, w_scales, q)
        nc.sync.dma_start(out=tz_sb[:], in_=tz.rearrange("(h p) c -> p h c", p=P))
        nc.sync.dma_start(list3[:], offs3)
        nc.sync.dma_start(out=wb_sb[:].bitcast(I32), in_=wb_words[0].rearrange("p n t -> p (n t)").bitcast(I32))
        for q in range(4):
            load_scale_rows(nc.sync, wb_sc, wb_scales, q)
        nc.gpsimd.dma_start(out=fk_sb[:], in_=fk.rearrange("(p t) o -> p (t o)", t=PACK))
        for q in range(2):
            load_scale_rows(nc.gpsimd, sx_sc, sx_scales, q)

        last = PACK - 1
        first = [sb.tile([P, J], F32, name=f"first{t}") for t in range(PACK)]
        second = [sb.tile([P, J], F32, name=f"second{t}") for t in range(PACK)]
        for t in range(PACK):
            nc.scalar.activation(second[t][:], x_plane[t][:].indirect(list2[:]), ACT.Copy)
            if t < last:
                nc.vector.tensor_copy(first[t][:], x_plane[t][:].indirect(list1[:]))
            else:
                nc.scalar.activation(first[t][:], x_plane[t][:].indirect(list1[:]), ACT.Copy)
        w2_sc = sb.tile([P, PACK, P], U8, name="w2_sc", align_bytes=64)
        deal(nc.vector.tensor_copy, w2_sc[:], w2s_raw[:], 16)
        gap = sb.tile([P, PACK, J], F32, name="gap", tag="w2s_raw", align_bytes=64)
        for t in range(last):
            nc.vector.tensor_tensor(gap[:, t, :], first[t][:], second[t][:], ALU.subtract)
        for cols in halves:
            nc.vector.tensor_tensor(gap[:, last, cols], first[last][:, cols], second[last][:, cols], ALU.subtract)
        w2_sb = sb.tile([P, PACK, P], U32, name="w2_sb", align_bytes=64)
        w_sb = sb.tile([P, PACK, 2 * P], U8, name="w_sb", align_bytes=64)
        deal(nc.scalar.copy, w2_sb[:], w2_raw[:], 4)
        deal(nc.scalar.copy, w_sb[:].bitcast(U16), w_raw[:].bitcast(U16), 8)

        u_grouped = sb.tile([P, J, PACK], BF16, name="u_grouped", align_bytes=64)
        u_codes = sb.tile([P, J], U32, name="u_codes", align_bytes=64)
        u_sc = sb.tile([P, J], U8, name="u_sc", align_bytes=64)
        for cols in halves:
            nc.vector.tensor_tensor(
                u_grouped[:, cols, :].rearrange("p (c i) t -> p c t i", i=4),
                gap[:, :, cols].rearrange("p t (c i) -> p c t i", i=4),
                fk_sb[:].unsqueeze(1).unsqueeze(3).broadcast_to([P, HALF // 4, PACK, 4]),
                ALU.mult,
            )
        for cols in halves:
            quantize(nc, u_codes, u_sc, u_grouped, cols, E4M3)
        w_sc = sb.tile([P, PACK, P], U8, name="w_sc", align_bytes=64)
        deal(nc.vector.tensor_copy, w_sc[:], ws_raw[:], 16)

        a_bank = [ps.tile([P, J], F32, name=f"a{t}") for t in range(PACK)]
        for t in range(PACK):
            nc.tensor.matmul_mx(
                out=a_bank[t][:], lhsT=w2_sb[:, t, :].bitcast(E5M2), lhsT_scale=w2_sc[:, t, :],
                rhs=sx_sb[:].bitcast(E4M3), rhs_scale=sx_sc[:], start=True, stop=False,
            )
        for t in range(PACK):
            for g, cols in enumerate(halves):
                nc.tensor.matmul_mx(
                    out=a_bank[t][:, cols], lhsT=w_sb[:, t, :].bitcast(E2M1), lhsT_scale=w_sc[:, t, :],
                    rhs=u_codes[:, cols].bitcast(E4M3), rhs_scale=u_sc[:, cols], start=False, stop=(g == 1),
                )

        scaled = sb.tile([P, PACK, J], F32, name="scaled")
        cut = [sb.tile([P, 1], F32, name=f"cut{t}") for t in range(PACK)]
        h_planes = sb.tile([P, PACK, J], BF16, name="h_planes")
        for t in range(PACK):
            nc.vector.tensor_scalar(scaled[:, t, :], a_bank[t][:], -0.4, None, ALU.mult, ALU.min, accum_out=cut[t][:])
        for t in range(2):
            nc.scalar.activation(h_planes[:, t, :], a_bank[t][:], ACT.Relu, bias=cut[t][:])
        nc.vector.tensor_scalar(h_planes[:, 2, :], a_bank[2][:], cut[2][:], 0.0, ALU.add, ALU.max)
        for cols in halves:
            nc.vector.tensor_scalar(h_planes[:, last, cols], a_bank[last][:, cols], cut[last][:], 0.0, ALU.add, ALU.max)

        picked = sb.tile([P, 2, J], F32, name="picked")
        for h in range(2):
            nc.scalar.activation(picked[:, h, :], tz_sb[:, h, :].indirect(list3[:]), ACT.Copy)

        h_grouped = sb.tile([P, J, PACK], BF16, name="h_grouped", align_bytes=64)
        h_codes = sb.tile([P, J], U32, name="h_codes", align_bytes=64)
        h_sc = sb.tile([P, J], U8, name="h_sc", align_bytes=64)
        for cols in halves:
            interleave(nc, h_grouped, h_planes, cols)
        for cols in halves:
            quantize(nc, h_codes, h_sc, h_grouped, cols, E5M2)

        out_rows = out.rearrange("(h p) j -> p h j", p=P)
        for g, cols in enumerate(halves):
            p_bank = ps.tile([P, 2, HALF], F32, name=f"p{g}")
            for h in range(2):
                nc.tensor.matmul_mx(
                    out=p_bank[:, h, :], lhsT=wb_sb[:, h * P : (h + 1) * P].bitcast(E5M2), lhsT_scale=wb_sc[:, h * P : (h + 1) * P],
                    rhs=h_codes[:, cols].bitcast(E5M2), rhs_scale=h_sc[:, cols], start=True, stop=True,
                )
            y = sb.tile([P, 2, HALF], F32, name=f"y{g}")
            nc.vector.tensor_tensor(y[:], p_bank[:], picked[:, :, cols], ALU.mult)
            nc.sync.dma_start(out=out_rows[:, :, cols], in_=y[:])
